import numpy as np
import ml_dtypes


def mxq(x, axis, fmt="e4m3"):
    dtype, down = {"e4m3": (ml_dtypes.float8_e4m3fn, 7), "e5m2": (ml_dtypes.float8_e5m2, 14)}[fmt]
    v = np.moveaxis(np.asarray(x, np.float32).astype(ml_dtypes.bfloat16).astype(np.float64), axis, -1)
    blocks = v.reshape(v.shape[:-1] + (-1, 32))
    amax = np.abs(blocks).max(-1, keepdims=True)
    byte = np.maximum(np.where(amax > 0, np.frexp(amax)[1] - 1 + 127, 0) - down, 1)
    scale = np.exp2(byte - 127.0)
    codes = (blocks / scale).astype(np.float32).astype(dtype).astype(np.float64)
    return np.moveaxis((codes * scale).reshape(v.shape), -1, axis)


WIDE = False


def mx_kscale(k):
    if not WIDE:
        return np.ones(k)
    levels = np.array([10, -10, 5, -5, 0])
    if k % 512:
        return np.exp2(np.random.permutation(np.resize(levels, k // 32))).repeat(32)
    a = np.empty((k // 512, 16))
    for p in range(k // 512):
        a[p, :8] = np.random.permutation(np.resize(levels, 8))
        for g in range(8):
            far = levels[np.abs(levels - a[p, g]) >= 10]
            a[p, g + 8] = far[np.random.randint(len(far))]
    return np.exp2(a.ravel()).repeat(32)


def f64(x):
    return np.asarray(x).astype(np.float64)


def striped(idx):
    return np.tile(np.asarray(idx).reshape(-1, 16).T, (8, 1)).astype(np.uint16)


def unstriped(offs):
    return offs[:16].T.reshape(-1).astype(np.int64)


E2M1 = np.array([0.0, 0.5, 1.0, 1.5, 2.0, 3.0, 4.0, 6.0, -0.0, -0.5, -1.0, -1.5, -2.0, -3.0, -4.0, -6.0])


def pack_weight(w, fmt):
    k, n = w.shape
    w = f64(np.asarray(w, np.float32).astype(ml_dtypes.bfloat16)).reshape(k // 32, 32, n)
    amax = np.abs(w).max(1)
    if fmt == "e4m3":
        byte = np.frexp(amax)[1] - 1 + 127 - 7
    else:
        mant, ex = np.frexp(amax / 6.0)
        byte = np.where(mant > 0.5, ex, ex - 1) + 127
    byte = np.clip(np.where(amax > 0, byte, 1), 1, 254)
    scaled = (w * np.exp2(127.0 - byte)[:, None, :]).reshape(k, n).astype(np.float32)
    by_word = np.ascontiguousarray(scaled.reshape(k // 512, 128, 4, n).transpose(0, 1, 3, 2))
    if fmt == "e4m3":
        words = by_word.astype(ml_dtypes.float8_e4m3fn).view(np.uint8)
    else:
        c = by_word.astype(ml_dtypes.float4_e2m1fn).view(np.uint8) & 0xF
        words = (c[..., 0::2] | (c[..., 1::2] << 4)).reshape(k // 512, 128, 2 * n)
    return np.ascontiguousarray(words), np.ascontiguousarray(byte.astype(np.uint8).reshape(k // 512, 16, n))


def unpack_weight(words, scales, fmt):
    g, _, n = scales.shape
    words = np.ascontiguousarray(words).reshape(g, 128, n, -1)
    if fmt == "e4m3":
        vals = words.view(ml_dtypes.float8_e4m3fn).astype(np.float64)
    else:
        nib = np.empty((g, 128, n, 4), np.uint8)
        nib[..., 0::2] = words & 0xF
        nib[..., 1::2] = words >> 4
        vals = E2M1[nib]
    vals = vals * np.repeat(np.exp2(scales.astype(np.float64) - 127.0), 8, axis=1)[..., None]
    return vals.transpose(0, 1, 3, 2).reshape(g * 512, n)


K, R, F, T, J, G = 512, 128, 512, 2048, 512, 64


def setup_inputs():
    n = np.random.standard_normal
    idx = np.random.permutation(T)[:J]
    fk = mx_kscale(K)
    ff = mx_kscale(F)
    tabp = pack_weight(n((K, T)) / fk[:, None], "e4m3")
    return {
        "tab_words": tabp[0],
        "tab_scales": tabp[1],
        "w1": (n((K, R)) * 1 / np.sqrt(K) * fk[:, None]).astype(np.float32),
        "share": (np.random.uniform(0.3, 1.2, (R, 1))).astype(np.float32),
        "wo": (n((F, R)) * 1 / np.sqrt(F) * ff[:, None]).astype(np.float32),
        "dy": (n((F, G)) / ff[:, None]).astype(np.float32),
        "old": (0.5 * n((R, J))).astype(np.float32),
        "offs": striped(idx),
    }


def reference(tab_words, tab_scales, w1, share, wo, dy, old, offs):
    idx = unstriped(offs)
    tabu = unpack_weight(tab_words, tab_scales, "e4m3")
    w1q = mxq(f64(w1), 0, "e4m3")
    tabidxg = tabu[:, idx]
    a = w1q.T @ tabidxg
    m1 = a.reshape(R, G, J // G).mean(axis=2)
    v1 = np.sqrt(np.square(a).reshape(R, G, J // G).mean(axis=2) - np.square(m1) + 0.05)
    u1 = np.tanh(v1 + m1 * f64(share))
    woq = mxq(f64(wo), 0, "e4m3")
    dyq = mxq(f64(dy), 0, "e4m3")
    c0 = woq.T @ dyq
    dv1 = c0 * (1.0 - np.square(u1))
    e1 = dv1 * 0.5 / np.sqrt(np.square(a).reshape(R, G, J // G).mean(axis=2) - np.square(m1) + 0.05) / 8.0
    r1 = np.repeat(e1, J // G, axis=1)
    dm1 = c0 * (1.0 - np.square(u1)) * f64(share) + dv1 * 0.5 / np.sqrt(np.square(a).reshape(R, G, J // G).mean(axis=2) - np.square(m1) + 0.05) * (-1.0) * m1 * 2.0
    e2 = dm1 / 8.0
    r2 = np.repeat(e2, J // G, axis=1)
    da = r1 * a * 2.0 + r2
    y = da + f64(old)
    return y

@@ -1,0 +1,152 @@
+from contextlib import ExitStack
+
+import concourse.mybir as mybir
+
+K, R, F, T, J, G = 512, 128, 512, 2048, 512, 64
+FLOPS = 2 * K * R * J + 2 * F * R * G
+
+F32 = mybir.dt.float32
+BF16 = mybir.dt.bfloat16
+I32 = mybir.dt.int32
+U32 = mybir.dt.uint32
+U16 = mybir.dt.uint16
+U8 = mybir.dt.uint8
+FP8X4 = mybir.dt.float8_e4m3fn_x4
+ALU = mybir.AluOpType
+ACT = mybir.ActivationFunctionType
+
+P = 128
+PACK = 4
+S = J // G
+HALVES = 2
+JH = J // HALVES
+GH = G // HALVES
+EPS = 0.05
+
+
+def tile_attend_cspreadpool_kernel(tc, tab_words, tab_scales, w1, share, wo, dy, old, offs, out):
+    nc = tc.nc
+    with ExitStack() as ctx:
+        keep = ctx.enter_context(tc.tile_pool(name="keep", bufs=1))
+        psum = ctx.enter_context(tc.psum_pool(name="psum", bufs=1))
+
+        def spread(t, h):
+            return t[:, h * GH : (h + 1) * GH].unsqueeze(2).to_broadcast([P, GH, S])
+
+        def grouped(ap):
+            return ap.rearrange("p (g s) -> p g s", s=S)
+
+        offsets = keep.tile([P, J // 16], U16, name="offsets")
+        nc.sync.dma_start(offsets[:], offs)
+
+        tab_s = keep.tile([P, T], U8, name="tab_s", tag="late_old", align_bytes=64)
+        nc.vector.memset(tab_s[:].bitcast(I32), 0)
+        w1_raw = keep.tile([P, PACK, R], F32, name="w1_raw", tag="raw")
+        nc.sync.dma_start(w1_raw[:], w1.rearrange("(p t) r -> p t r", t=PACK))
+        for r in range(4):
+            nc.sync.dma_start(tab_s[r:P:32, :].bitcast(I32), tab_scales[0][r:16:4, :].bitcast(I32))
+        tab_w = keep.tile([P, T], U32, name="tab_w")
+        nc.sync.dma_start(tab_w[:].bitcast(I32), tab_words[0].rearrange("p c t -> p (c t)").bitcast(I32))
+        dy_raw = keep.tile([P, PACK, G], F32, name="dy_raw")
+        nc.sync.dma_start(dy_raw[:], dy.rearrange("(p t) g -> p t g", t=PACK))
+
+        warm_in = keep.tile([P, 1], F32, name="warm_in")
+        warm_out = keep.tile([P, 1], F32, name="warm_out")
+        nc.vector.memset(warm_in[:], 1.0)
+        nc.scalar.activation(warm_out[:], warm_in[:], ACT.Abs_reciprocal_sqrt)
+
+        def cast(raw, width, name):
+            b = keep.tile([P, width, PACK], BF16, name=name + "_b", align_bytes=64)
+            nc.scalar.copy(b[:], raw[:].rearrange("p t w -> p w t"))
+            return b
+
+        def quant(b, width, name, tag):
+            codes = keep.tile([P, width], U32, name=name + "_c", tag=tag, align_bytes=64)
+            scales = keep.tile([P, width], U8, name=name + "_s", align_bytes=64)
+            nc.vector.quantize_mx(codes[:].bitcast(FP8X4), scales[:], b[:].rearrange("p w t -> p (w t)"))
+            return codes, scales
+
+        w1_b = cast(w1_raw, R, "w1")
+        got_s = keep.tile([P, J], U8, name="got_s", align_bytes=64)
+        nc.vector.tensor_copy(got_s[:], tab_s[:].indirect(offsets[:]))
+        w1_c, w1_s = quant(w1_b, R, "w1", "w1_c")
+
+        wo_raw = keep.tile([P, PACK, R], F32, name="wo_raw", tag="raw")
+        nc.sync.dma_start(wo_raw[:], wo.rearrange("(p t) r -> p t r", t=PACK))
+        old_t = keep.tile([P, J], F32, name="old_t", tag="late_old", align_bytes=64)
+        nc.sync.dma_start(old_t[:], old)
+        share_t = keep.tile([P, 1], F32, name="share_t")
+        nc.sync.dma_start(share_t[:], share)
+
+        a_ps = []
+        for h in range(HALVES):
+            got_w = keep.tile([P, JH], U32, name="got_w%d" % h, align_bytes=64)
+            nc.vector.tensor_copy(got_w[:], tab_w[:].indirect(offsets[:, h * JH // 16 : (h + 1) * JH // 16]))
+            bank = psum.tile([P, JH], F32, name="a_ps%d" % h)
+            nc.tensor.matmul_mx(
+                bank[:], lhsT=w1_c[:].bitcast(FP8X4), lhsT_scale=w1_s[:],
+                rhs=got_w[:].bitcast(FP8X4), rhs_scale=got_s[:, h * JH : (h + 1) * JH], start=True, stop=True,
+            )
+            a_ps.append(bank)
+
+        trio = keep.tile([P, 3 * G], F32, name="trio")
+        s1, v8, neg_s1 = trio[:, 0:G], trio[:, G : 2 * G], trio[:, 2 * G : 3 * G]
+        s2 = keep.tile([P, G], F32, name="s2", tag="s2", align_bytes=64)
+        sq = []
+        for h in range(HALVES):
+            nc.vector.tensor_reduce(s1[:, h * GH : (h + 1) * GH], grouped(a_ps[h][:]), mybir.AxisListType.X, ALU.add)
+            sq_h = keep.tile([P, JH], F32, name="sq%d" % h)
+            nc.scalar.activation(sq_h[:], a_ps[h][:], ACT.Square)
+            sq.append(sq_h)
+        s1sq = keep.tile([P, G], F32, name="s1sq", tag="s1sq", align_bytes=64)
+        nc.scalar.activation(s1sq[:], s1, ACT.Square)
+        nc.scalar.activation(neg_s1, s1, ACT.Copy, scale=-1.0)
+        for h in range(HALVES):
+            nc.vector.tensor_reduce(s2[:, h * GH : (h + 1) * GH], grouped(sq[h][:]), mybir.AxisListType.X, ALU.add)
+
+        wo_b = cast(wo_raw, R, "wo")
+        dy_b = cast(dy_raw, G, "dy")
+
+        dev = keep.tile([P, G], F32, name="dev")
+        nc.vector.scalar_tensor_tensor(dev[:], s2[:], float(S), s1sq[:], ALU.mult, ALU.subtract)
+        r8 = keep.tile([P, G], F32, name="r8")
+        nc.scalar.activation(r8[:], dev[:], ACT.Abs_reciprocal_sqrt, bias=EPS * S * S)
+        nc.vector.scalar_tensor_tensor(v8, dev[:], EPS * S * S, r8[:], ALU.add, ALU.mult)
+
+        wo_c, wo_s = quant(wo_b, R, "wo", "s1sq")
+        dy_c, dy_s = quant(dy_b, G, "dy", "s2")
+        c0 = psum.tile([P, G], F32, name="c0")
+        nc.tensor.matmul_mx(
+            c0[:], lhsT=wo_c[:].bitcast(FP8X4), lhsT_scale=wo_s[:],
+            rhs=dy_c[:].bitcast(FP8X4), rhs_scale=dy_s[:], start=True, stop=True,
+        )
+
+        zh = keep.tile([P, 2 * G], F32, name="zh")
+        z8, h8 = zh[:, 0:G], zh[:, G : 2 * G]
+        nc.vector.scalar_tensor_tensor(zh[:], trio[:, 0 : 2 * G], share_t[:], trio[:, G : 3 * G], ALU.mult, ALU.add)
+        u = keep.tile([P, G], F32, name="u")
+        nc.scalar.activation(u[:], z8, ACT.Tanh, scale=1.0 / S)
+        u2 = keep.tile([P, G], F32, name="u2")
+        nc.scalar.activation(u2[:], u[:], ACT.Square)
+
+        cr = keep.tile([P, G], F32, name="cr")
+        nc.vector.tensor_tensor(cr[:], c0[:], r8[:], ALU.mult)
+        y, w, nda = [], [], []
+        for h in range(HALVES):
+            y.append(keep.tile([P, JH], F32, name="y%d" % h))
+            nc.vector.scalar_tensor_tensor(
+                grouped(y[h][:]), spread(h8, h), 1.0 / S, grouped(a_ps[h][:]), ALU.mult, ALU.add
+            )
+        for h in range(HALVES):
+            w.append(keep.tile([P, JH], F32, name="w%d" % h))
+            nc.vector.tensor_tensor(grouped(w[h][:]), grouped(y[h][:]), spread(cr, h), ALU.mult)
+        for h in range(HALVES):
+            nda.append(keep.tile([P, JH], F32, name="nda%d" % h))
+            nc.vector.scalar_tensor_tensor(
+                grouped(nda[h][:]), spread(u2, h), 1.0, grouped(w[h][:]), ALU.subtract, ALU.mult
+            )
+        for h in range(HALVES):
+            cols = slice(h * JH, (h + 1) * JH)
+            res = keep.tile([P, JH], F32, name="res%d" % h)
+            nc.vector.tensor_tensor(res[:], old_t[:, cols], nda[h][:], ALU.subtract)
+            nc.sync.dma_start(out[:, cols], res[:])

@@ -22,6 +22,7 @@ HALVES = 2
 JH = J // HALVES
 GH = G // HALVES
 EPS = 0.05
+EARLY = 512
 
 
 def tile_attend_cspreadpool_kernel(tc, tab_words, tab_scales, w1, share, wo, dy, old, offs, out):
@@ -43,10 +44,12 @@ def tile_attend_cspreadpool_kernel(tc, tab_words, tab_scales, w1, share, wo, dy,
         nc.vector.memset(tab_s[:].bitcast(I32), 0)
         w1_raw = keep.tile([P, PACK, R], F32, name="w1_raw", tag="raw")
         nc.sync.dma_start(w1_raw[:], w1.rearrange("(p t) r -> p t r", t=PACK))
+        tab_w = keep.tile([P, T], U32, name="tab_w")
+        words = tab_words[0].rearrange("p c t -> p (c t)").bitcast(I32)
+        nc.sync.dma_start(tab_w[:, 0:EARLY].bitcast(I32), words[:, 0:EARLY])
         for r in range(4):
             nc.sync.dma_start(tab_s[r:P:32, :].bitcast(I32), tab_scales[0][r:16:4, :].bitcast(I32))
-        tab_w = keep.tile([P, T], U32, name="tab_w")
-        nc.sync.dma_start(tab_w[:].bitcast(I32), tab_words[0].rearrange("p c t -> p (c t)").bitcast(I32))
+        nc.sync.dma_start(tab_w[:, EARLY:T].bitcast(I32), words[:, EARLY:T])
         dy_raw = keep.tile([P, PACK, G], F32, name="dy_raw")
         nc.sync.dma_start(dy_raw[:], dy.rearrange("(p t) g -> p t g", t=PACK))
 
@@ -55,8 +58,8 @@ def tile_attend_cspreadpool_kernel(tc, tab_words, tab_scales, w1, share, wo, dy,
         nc.vector.memset(warm_in[:], 1.0)
         nc.scalar.activation(warm_out[:], warm_in[:], ACT.Abs_reciprocal_sqrt)
 
-        def cast(raw, width, name):
-            b = keep.tile([P, width, PACK], BF16, name=name + "_b", align_bytes=64)
+        def cast(raw, width, name, tag):
+            b = keep.tile([P, width, PACK], BF16, name=name + "_b", tag=tag, align_bytes=64)
             nc.scalar.copy(b[:], raw[:].rearrange("p t w -> p w t"))
             return b
 
@@ -66,8 +69,8 @@ def tile_attend_cspreadpool_kernel(tc, tab_words, tab_scales, w1, share, wo, dy,
             nc.vector.quantize_mx(codes[:].bitcast(FP8X4), scales[:], b[:].rearrange("p w t -> p (w t)"))
             return codes, scales
 
-        w1_b = cast(w1_raw, R, "w1")
-        got_s = keep.tile([P, J], U8, name="got_s", align_bytes=64)
+        w1_b = cast(w1_raw, R, "w1", "w1_b")
+        got_s = keep.tile([P, J], U8, name="got_s", tag="got_s", align_bytes=64)
         nc.vector.tensor_copy(got_s[:], tab_s[:].indirect(offsets[:]))
         w1_c, w1_s = quant(w1_b, R, "w1", "w1_c")
 
@@ -80,7 +83,7 @@ def tile_attend_cspreadpool_kernel(tc, tab_words, tab_scales, w1, share, wo, dy,
 
         a_ps = []
         for h in range(HALVES):
-            got_w = keep.tile([P, JH], U32, name="got_w%d" % h, align_bytes=64)
+            got_w = keep.tile([P, JH], U32, name="got_w%d" % h, tag="got_w%d" % h, align_bytes=64)
             nc.vector.tensor_copy(got_w[:], tab_w[:].indirect(offsets[:, h * JH // 16 : (h + 1) * JH // 16]))
             bank = psum.tile([P, JH], F32, name="a_ps%d" % h)
             nc.tensor.matmul_mx(
@@ -89,29 +92,38 @@ def tile_attend_cspreadpool_kernel(tc, tab_words, tab_scales, w1, share, wo, dy,
             )
             a_ps.append(bank)
 
-        trio = keep.tile([P, 3 * G], F32, name="trio")
-        s1, v8, neg_s1 = trio[:, 0:G], trio[:, G : 2 * G], trio[:, 2 * G : 3 * G]
+        s1 = keep.tile([P, G], F32, name="s1")
         s2 = keep.tile([P, G], F32, name="s2", tag="s2", align_bytes=64)
         sq = []
         for h in range(HALVES):
-            nc.vector.tensor_reduce(s1[:, h * GH : (h + 1) * GH], grouped(a_ps[h][:]), mybir.AxisListType.X, ALU.add)
-            sq_h = keep.tile([P, JH], F32, name="sq%d" % h)
-            nc.scalar.activation(sq_h[:], a_ps[h][:], ACT.Square)
-            sq.append(sq_h)
-        s1sq = keep.tile([P, G], F32, name="s1sq", tag="s1sq", align_bytes=64)
-        nc.scalar.activation(s1sq[:], s1, ACT.Square)
-        nc.scalar.activation(neg_s1, s1, ACT.Copy, scale=-1.0)
+            sq.append(keep.tile([P, JH], F32, name="sq%d" % h))
+            nc.scalar.activation(sq[h][:], a_ps[h][:], ACT.Square)
+        wo_b = cast(wo_raw, R, "wo", "got_w1")
+        dy_b = cast(dy_raw, G, "dy", "got_s")
         for h in range(HALVES):
+            nc.vector.tensor_reduce(s1[:, h * GH : (h + 1) * GH], grouped(a_ps[h][:]), mybir.AxisListType.X, ALU.add)
             nc.vector.tensor_reduce(s2[:, h * GH : (h + 1) * GH], grouped(sq[h][:]), mybir.AxisListType.X, ALU.add)
-
-        wo_b = cast(wo_raw, R, "wo")
-        dy_b = cast(dy_raw, G, "dy")
+        s1sq = keep.tile([P, G], F32, name="s1sq", tag="s1sq", align_bytes=64)
+        nc.scalar.activation(s1sq[:], s1[:], ACT.Square)
 
         dev = keep.tile([P, G], F32, name="dev")
         nc.vector.scalar_tensor_tensor(dev[:], s2[:], float(S), s1sq[:], ALU.mult, ALU.subtract)
         r8 = keep.tile([P, G], F32, name="r8")
         nc.scalar.activation(r8[:], dev[:], ACT.Abs_reciprocal_sqrt, bias=EPS * S * S)
-        nc.vector.scalar_tensor_tensor(v8, dev[:], EPS * S * S, r8[:], ALU.add, ALU.mult)
+
+        xc, xn, w, nda = [], [], [], []
+        for h in range(HALVES):
+            xc.append(keep.tile([P, JH], F32, name="xc%d" % h))
+            nc.vector.scalar_tensor_tensor(
+                grouped(xc[h][:]), grouped(a_ps[h][:]), float(S), spread(s1, h), ALU.mult, ALU.subtract
+            )
+
+        v8 = keep.tile([P, G], F32, name="v8")
+        nc.vector.scalar_tensor_tensor(v8[:], dev[:], EPS * S * S, r8[:], ALU.add, ALU.mult)
+        z8 = keep.tile([P, G], F32, name="z8")
+        nc.vector.scalar_tensor_tensor(z8[:], s1[:], share_t[:], v8[:], ALU.mult, ALU.add)
+        u = keep.tile([P, G], F32, name="u")
+        nc.scalar.activation(u[:], z8[:], ACT.Tanh, scale=1.0 / S)
 
         wo_c, wo_s = quant(wo_b, R, "wo", "s1sq")
         dy_c, dy_s = quant(dy_b, G, "dy", "s2")
@@ -121,25 +133,16 @@ def tile_attend_cspreadpool_kernel(tc, tab_words, tab_scales, w1, share, wo, dy,
             rhs=dy_c[:].bitcast(FP8X4), rhs_scale=dy_s[:], start=True, stop=True,
         )
 
-        zh = keep.tile([P, 2 * G], F32, name="zh")
-        z8, h8 = zh[:, 0:G], zh[:, G : 2 * G]
-        nc.vector.scalar_tensor_tensor(zh[:], trio[:, 0 : 2 * G], share_t[:], trio[:, G : 3 * G], ALU.mult, ALU.add)
-        u = keep.tile([P, G], F32, name="u")
-        nc.scalar.activation(u[:], z8, ACT.Tanh, scale=1.0 / S)
-        u2 = keep.tile([P, G], F32, name="u2")
-        nc.scalar.activation(u2[:], u[:], ACT.Square)
-
-        cr = keep.tile([P, G], F32, name="cr")
-        nc.vector.tensor_tensor(cr[:], c0[:], r8[:], ALU.mult)
-        y, w, nda = [], [], []
         for h in range(HALVES):
-            y.append(keep.tile([P, JH], F32, name="y%d" % h))
-            nc.vector.scalar_tensor_tensor(
-                grouped(y[h][:]), spread(h8, h), 1.0 / S, grouped(a_ps[h][:]), ALU.mult, ALU.add
-            )
+            xn.append(keep.tile([P, JH], F32, name="xn%d" % h))
+            nc.vector.tensor_tensor(grouped(xn[h][:]), grouped(xc[h][:]), spread(r8, h), ALU.mult)
         for h in range(HALVES):
             w.append(keep.tile([P, JH], F32, name="w%d" % h))
-            nc.vector.tensor_tensor(grouped(w[h][:]), grouped(y[h][:]), spread(cr, h), ALU.mult)
+            nc.vector.scalar_tensor_tensor(
+                grouped(w[h][:]), grouped(xn[h][:]), share_t[:], spread(c0, h), ALU.add, ALU.mult
+            )
+        u2 = keep.tile([P, G], F32, name="u2")
+        nc.vector.tensor_tensor(u2[:], u[:], u[:], ALU.mult)
         for h in range(HALVES):
             nda.append(keep.tile([P, JH], F32, name="nda%d" % h))
             nc.vector.scalar_tensor_tensor(
@@ -148,5 +151,5 @@ def tile_attend_cspreadpool_kernel(tc, tab_words, tab_scales, w1, share, wo, dy,
         for h in range(HALVES):
             cols = slice(h * JH, (h + 1) * JH)
             res = keep.tile([P, JH], F32, name="res%d" % h)
-            nc.vector.tensor_tensor(res[:], old_t[:, cols], nda[h][:], ALU.subtract)
+            nc.vector.scalar_tensor_tensor(res[:], nda[h][:], -1.0 / S, old_t[:, cols], ALU.mult, ALU.add)
             nc.sync.dma_start(out[:, cols], res[:])

@@ -22,7 +22,6 @@ HALVES = 2
 JH = J // HALVES
 GH = G // HALVES
 EPS = 0.05
-EARLY = 512
 
 
 def tile_attend_cspreadpool_kernel(tc, tab_words, tab_scales, w1, share, wo, dy, old, offs, out):
@@ -38,7 +37,6 @@ def tile_attend_cspreadpool_kernel(tc, tab_words, tab_scales, w1, share, wo, dy,
             return ap.rearrange("p (g s) -> p g s", s=S)
 
         offsets = keep.tile([P, J // 16], U16, name="offsets")
-        nc.sync.dma_start(offsets[:], offs)
 
         tab_s = keep.tile([P, T], U8, name="tab_s", tag="late_old", align_bytes=64)
         nc.vector.memset(tab_s[:].bitcast(I32), 0)
@@ -46,10 +44,10 @@ def tile_attend_cspreadpool_kernel(tc, tab_words, tab_scales, w1, share, wo, dy,
         nc.sync.dma_start(w1_raw[:], w1.rearrange("(p t) r -> p t r", t=PACK))
         tab_w = keep.tile([P, T], U32, name="tab_w")
         words = tab_words[0].rearrange("p c t -> p (c t)").bitcast(I32)
-        nc.sync.dma_start(tab_w[:, 0:EARLY].bitcast(I32), words[:, 0:EARLY])
+        nc.sync.dma_start(offsets[:], offs)
         for r in range(4):
             nc.sync.dma_start(tab_s[r:P:32, :].bitcast(I32), tab_scales[0][r:16:4, :].bitcast(I32))
-        nc.sync.dma_start(tab_w[:, EARLY:T].bitcast(I32), words[:, EARLY:T])
+        nc.sync.dma_start(tab_w[:].bitcast(I32), words)
         dy_raw = keep.tile([P, PACK, G], F32, name="dy_raw")
         nc.sync.dma_start(dy_raw[:], dy.rearrange("(p t) g -> p t g", t=PACK))
 
@@ -96,10 +94,10 @@ def tile_attend_cspreadpool_kernel(tc, tab_words, tab_scales, w1, share, wo, dy,
         s2 = keep.tile([P, G], F32, name="s2", tag="s2", align_bytes=64)
         sq = []
         for h in range(HALVES):
-            sq.append(keep.tile([P, JH], F32, name="sq%d" % h))
+            sq.append(keep.tile([P, JH], F32, name="sq%d" % h, tag="sq%d" % h, align_bytes=64))
             nc.scalar.activation(sq[h][:], a_ps[h][:], ACT.Square)
         wo_b = cast(wo_raw, R, "wo", "got_w1")
-        dy_b = cast(dy_raw, G, "dy", "got_s")
+        dy_b = cast(dy_raw, G, "dy", "dy_b")
         for h in range(HALVES):
             nc.vector.tensor_reduce(s1[:, h * GH : (h + 1) * GH], grouped(a_ps[h][:]), mybir.AxisListType.X, ALU.add)
             nc.vector.tensor_reduce(s2[:, h * GH : (h + 1) * GH], grouped(sq[h][:]), mybir.AxisListType.X, ALU.add)
@@ -111,11 +109,12 @@ def tile_attend_cspreadpool_kernel(tc, tab_words, tab_scales, w1, share, wo, dy,
         r8 = keep.tile([P, G], F32, name="r8")
         nc.scalar.activation(r8[:], dev[:], ACT.Abs_reciprocal_sqrt, bias=EPS * S * S)
 
-        xc, xn, w, nda = [], [], [], []
+        xn, w, nda = [], [], []
+        xc_all = keep.tile([P, J], F32, name="xc_all", tag="s2", align_bytes=64)
+        xc = [xc_all[:, h * JH : (h + 1) * JH] for h in range(HALVES)]
         for h in range(HALVES):
-            xc.append(keep.tile([P, JH], F32, name="xc%d" % h))
             nc.vector.scalar_tensor_tensor(
-                grouped(xc[h][:]), grouped(a_ps[h][:]), float(S), spread(s1, h), ALU.mult, ALU.subtract
+                grouped(xc[h]), grouped(a_ps[h][:]), float(S), spread(s1, h), ALU.mult, ALU.subtract
             )
 
         v8 = keep.tile([P, G], F32, name="v8")
@@ -126,7 +125,7 @@ def tile_attend_cspreadpool_kernel(tc, tab_words, tab_scales, w1, share, wo, dy,
         nc.scalar.activation(u[:], z8[:], ACT.Tanh, scale=1.0 / S)
 
         wo_c, wo_s = quant(wo_b, R, "wo", "s1sq")
-        dy_c, dy_s = quant(dy_b, G, "dy", "s2")
+        dy_c, dy_s = quant(dy_b, G, "dy", "dy_c")
         c0 = psum.tile([P, G], F32, name="c0")
         nc.tensor.matmul_mx(
             c0[:], lhsT=wo_c[:].bitcast(FP8X4), lhsT_scale=wo_s[:],
@@ -135,7 +134,7 @@ def tile_attend_cspreadpool_kernel(tc, tab_words, tab_scales, w1, share, wo, dy,
 
         for h in range(HALVES):
             xn.append(keep.tile([P, JH], F32, name="xn%d" % h))
-            nc.vector.tensor_tensor(grouped(xn[h][:]), grouped(xc[h][:]), spread(r8, h), ALU.mult)
+            nc.vector.tensor_tensor(grouped(xn[h][:]), grouped(xc[h]), spread(r8, h), ALU.mult)
         for h in range(HALVES):
             w.append(keep.tile([P, JH], F32, name="w%d" % h))
             nc.vector.scalar_tensor_tensor(

@@ -53,7 +53,7 @@ def tile_attend_cspreadpool_kernel(tc, tab_words, tab_scales, w1, share, wo, dy,
 
         warm_in = keep.tile([P, 1], F32, name="warm_in")
         warm_out = keep.tile([P, 1], F32, name="warm_out")
-        nc.vector.memset(warm_in[:], 1.0)
+        nc.vector.memset(warm_in[:], float(S * S))
         nc.scalar.activation(warm_out[:], warm_in[:], ACT.Abs_reciprocal_sqrt)
 
         def cast(raw, width, name, tag):
@@ -109,7 +109,8 @@ def tile_attend_cspreadpool_kernel(tc, tab_words, tab_scales, w1, share, wo, dy,
         r8 = keep.tile([P, G], F32, name="r8")
         nc.scalar.activation(r8[:], dev[:], ACT.Abs_reciprocal_sqrt, bias=EPS * S * S)
 
-        xn, w, nda = [], [], []
+        xn = []
+        w = keep.tile([P, J], F32, name="w")
         xc_all = keep.tile([P, J], F32, name="xc_all", tag="s2", align_bytes=64)
         xc = [xc_all[:, h * JH : (h + 1) * JH] for h in range(HALVES)]
         for h in range(HALVES):
@@ -122,7 +123,7 @@ def tile_attend_cspreadpool_kernel(tc, tab_words, tab_scales, w1, share, wo, dy,
         z8 = keep.tile([P, G], F32, name="z8")
         nc.vector.scalar_tensor_tensor(z8[:], s1[:], share_t[:], v8[:], ALU.mult, ALU.add)
         u = keep.tile([P, G], F32, name="u")
-        nc.scalar.activation(u[:], z8[:], ACT.Tanh, scale=1.0 / S)
+        nc.scalar.activation(u[:], z8[:], ACT.Tanh, scale=warm_out[:])
 
         wo_c, wo_s = quant(wo_b, R, "wo", "s1sq")
         dy_c, dy_s = quant(dy_b, G, "dy", "dy_c")
@@ -136,19 +137,32 @@ def tile_attend_cspreadpool_kernel(tc, tab_words, tab_scales, w1, share, wo, dy,
             xn.append(keep.tile([P, JH], F32, name="xn%d" % h))
             nc.vector.tensor_tensor(grouped(xn[h][:]), grouped(xc[h]), spread(r8, h), ALU.mult)
         for h in range(HALVES):
-            w.append(keep.tile([P, JH], F32, name="w%d" % h))
             nc.vector.scalar_tensor_tensor(
-                grouped(w[h][:]), grouped(xn[h][:]), share_t[:], spread(c0, h), ALU.add, ALU.mult
+                grouped(w[:, h * JH : (h + 1) * JH]), grouped(xn[h][:]), share_t[:], spread(c0, h), ALU.add, ALU.mult
             )
         u2 = keep.tile([P, G], F32, name="u2")
         nc.vector.tensor_tensor(u2[:], u[:], u[:], ALU.mult)
-        for h in range(HALVES):
-            nda.append(keep.tile([P, JH], F32, name="nda%d" % h))
+        pieces = [(0, 24), (24, 24), (48, 16)]
+        nda = keep.tile([P, J], F32, name="nda")
+
+        def gradient(n):
+            g0, ng = pieces[n]
+            cols = slice(g0 * S, (g0 + ng) * S)
             nc.vector.scalar_tensor_tensor(
-                grouped(nda[h][:]), spread(u2, h), 1.0, grouped(w[h][:]), ALU.subtract, ALU.mult
+                grouped(nda[:, cols]), u2[:, g0 : g0 + ng].unsqueeze(2).to_broadcast([P, ng, S]), 1.0,
+                grouped(w[:, cols]), ALU.subtract, ALU.mult,
             )
-        for h in range(HALVES):
-            cols = slice(h * JH, (h + 1) * JH)
-            res = keep.tile([P, JH], F32, name="res%d" % h)
-            nc.vector.scalar_tensor_tensor(res[:], nda[h][:], -1.0 / S, old_t[:, cols], ALU.mult, ALU.add)
+
+        def finish(n):
+            g0, ng = pieces[n]
+            cols = slice(g0 * S, (g0 + ng) * S)
+            res = keep.tile([P, ng * S], F32, name="res%d" % n)
+            nc.vector.scalar_tensor_tensor(res[:], nda[:, cols], -1.0 / S, old_t[:, cols], ALU.mult, ALU.add)
             nc.sync.dma_start(out[:, cols], res[:])
+
+        gradient(0)
+        gradient(1)
+        finish(0)
+        gradient(2)
+        finish(1)
+        finish(2)

from contextlib import ExitStack

import concourse.mybir as mybir

K, R, F, T, J, G = 512, 128, 512, 2048, 512, 64
FLOPS = 2 * K * R * J + 2 * F * R * G

F32 = mybir.dt.float32
BF16 = mybir.dt.bfloat16
I32 = mybir.dt.int32
U32 = mybir.dt.uint32
U16 = mybir.dt.uint16
U8 = mybir.dt.uint8
FP8X4 = mybir.dt.float8_e4m3fn_x4
ALU = mybir.AluOpType
ACT = mybir.ActivationFunctionType

P = 128
PACK = 4
S = J // G
HALVES = 2
JH = J // HALVES
GH = G // HALVES
EPS = 0.05


def tile_attend_cspreadpool_kernel(tc, tab_words, tab_scales, w1, share, wo, dy, old, offs, out):
    nc = tc.nc
    with ExitStack() as ctx:
        keep = ctx.enter_context(tc.tile_pool(name="keep", bufs=1))
        psum = ctx.enter_context(tc.psum_pool(name="psum", bufs=1))

        def spread(t, h):
            return t[:, h * GH : (h + 1) * GH].unsqueeze(2).to_broadcast([P, GH, S])

        def grouped(ap):
            return ap.rearrange("p (g s) -> p g s", s=S)

        offsets = keep.tile([P, J // 16], U16, name="offsets")

        tab_s = keep.tile([P, T], U8, name="tab_s", tag="late_old", align_bytes=64)
        nc.vector.memset(tab_s[:].bitcast(I32), 0)
        w1_raw = keep.tile([P, PACK, R], F32, name="w1_raw", tag="raw")
        nc.sync.dma_start(w1_raw[:], w1.rearrange("(p t) r -> p t r", t=PACK))
        tab_w = keep.tile([P, T], U32, name="tab_w")
        words = tab_words[0].rearrange("p c t -> p (c t)").bitcast(I32)
        nc.sync.dma_start(offsets[:], offs)
        for r in range(4):
            nc.sync.dma_start(tab_s[r:P:32, :].bitcast(I32), tab_scales[0][r:16:4, :].bitcast(I32))
        nc.sync.dma_start(tab_w[:].bitcast(I32), words)
        dy_raw = keep.tile([P, PACK, G], F32, name="dy_raw")
        nc.sync.dma_start(dy_raw[:], dy.rearrange("(p t) g -> p t g", t=PACK))

        warm_in = keep.tile([P, 1], F32, name="warm_in")
        warm_out = keep.tile([P, 1], F32, name="warm_out")
        nc.vector.memset(warm_in[:], float(S * S))
        nc.scalar.activation(warm_out[:], warm_in[:], ACT.Abs_reciprocal_sqrt)

        def cast(raw, width, name, tag):
            b = keep.tile([P, width, PACK], BF16, name=name + "_b", tag=tag, align_bytes=64)
            nc.scalar.copy(b[:], raw[:].rearrange("p t w -> p w t"))
            return b

        def quant(b, width, name, tag):
            codes = keep.tile([P, width], U32, name=name + "_c", tag=tag, align_bytes=64)
            scales = keep.tile([P, width], U8, name=name + "_s", align_bytes=64)
            nc.vector.quantize_mx(codes[:].bitcast(FP8X4), scales[:], b[:].rearrange("p w t -> p (w t)"))
            return codes, scales

        w1_b = cast(w1_raw, R, "w1", "w1_b")
        got_s = keep.tile([P, J], U8, name="got_s", tag="got_s", align_bytes=64)
        nc.vector.tensor_copy(got_s[:], tab_s[:].indirect(offsets[:]))
        w1_c, w1_s = quant(w1_b, R, "w1", "w1_c")

        wo_raw = keep.tile([P, PACK, R], F32, name="wo_raw", tag="raw")
        nc.sync.dma_start(wo_raw[:], wo.rearrange("(p t) r -> p t r", t=PACK))
        old_t = keep.tile([P, J], F32, name="old_t", tag="late_old", align_bytes=64)
        nc.sync.dma_start(old_t[:], old)
        share_t = keep.tile([P, 1], F32, name="share_t")
        nc.sync.dma_start(share_t[:], share)

        a_ps = []
        for h in range(HALVES):
            got_w = keep.tile([P, JH], U32, name="got_w%d" % h, tag="got_w%d" % h, align_bytes=64)
            nc.vector.tensor_copy(got_w[:], tab_w[:].indirect(offsets[:, h * JH // 16 : (h + 1) * JH // 16]))
            bank = psum.tile([P, JH], F32, name="a_ps%d" % h)
            nc.tensor.matmul_mx(
                bank[:], lhsT=w1_c[:].bitcast(FP8X4), lhsT_scale=w1_s[:],
                rhs=got_w[:].bitcast(FP8X4), rhs_scale=got_s[:, h * JH : (h + 1) * JH], start=True, stop=True,
            )
            a_ps.append(bank)

        s1 = keep.tile([P, G], F32, name="s1")
        s2 = keep.tile([P, G], F32, name="s2", tag="s2", align_bytes=64)
        sq = []
        for h in range(HALVES):
            sq.append(keep.tile([P, JH], F32, name="sq%d" % h, tag="sq%d" % h, align_bytes=64))
            nc.scalar.activation(sq[h][:], a_ps[h][:], ACT.Square)
        wo_b = cast(wo_raw, R, "wo", "got_w1")
        dy_b = cast(dy_raw, G, "dy", "dy_b")
        for h in range(HALVES):
            nc.vector.tensor_reduce(s1[:, h * GH : (h + 1) * GH], grouped(a_ps[h][:]), mybir.AxisListType.X, ALU.add)
            nc.vector.tensor_reduce(s2[:, h * GH : (h + 1) * GH], grouped(sq[h][:]), mybir.AxisListType.X, ALU.add)
        s1sq = keep.tile([P, G], F32, name="s1sq", tag="s1sq", align_bytes=64)
        nc.scalar.activation(s1sq[:], s1[:], ACT.Square)

        dev = keep.tile([P, G], F32, name="dev")
        nc.vector.scalar_tensor_tensor(dev[:], s2[:], float(S), s1sq[:], ALU.mult, ALU.subtract)
        r8 = keep.tile([P, G], F32, name="r8")
        nc.scalar.activation(r8[:], dev[:], ACT.Abs_reciprocal_sqrt, bias=EPS * S * S)

        xn = []
        w = keep.tile([P, J], F32, name="w")
        xc_all = keep.tile([P, J], F32, name="xc_all", tag="s2", align_bytes=64)
        xc = [xc_all[:, h * JH : (h + 1) * JH] for h in range(HALVES)]
        for h in range(HALVES):
            nc.vector.scalar_tensor_tensor(
                grouped(xc[h]), grouped(a_ps[h][:]), float(S), spread(s1, h), ALU.mult, ALU.subtract
            )

        v8 = keep.tile([P, G], F32, name="v8")
        nc.vector.scalar_tensor_tensor(v8[:], dev[:], EPS * S * S, r8[:], ALU.add, ALU.mult)
        z8 = keep.tile([P, G], F32, name="z8")
        nc.vector.scalar_tensor_tensor(z8[:], s1[:], share_t[:], v8[:], ALU.mult, ALU.add)
        u = keep.tile([P, G], F32, name="u")
        nc.scalar.activation(u[:], z8[:], ACT.Tanh, scale=warm_out[:])

        wo_c, wo_s = quant(wo_b, R, "wo", "s1sq")
        dy_c, dy_s = quant(dy_b, G, "dy", "dy_c")
        c0 = psum.tile([P, G], F32, name="c0")
        nc.tensor.matmul_mx(
            c0[:], lhsT=wo_c[:].bitcast(FP8X4), lhsT_scale=wo_s[:],
            rhs=dy_c[:].bitcast(FP8X4), rhs_scale=dy_s[:], start=True, stop=True,
        )

        for h in range(HALVES):
            xn.append(keep.tile([P, JH], F32, name="xn%d" % h))
            nc.vector.tensor_tensor(grouped(xn[h][:]), grouped(xc[h]), spread(r8, h), ALU.mult)
        for h in range(HALVES):
            nc.vector.scalar_tensor_tensor(
                grouped(w[:, h * JH : (h + 1) * JH]), grouped(xn[h][:]), share_t[:], spread(c0, h), ALU.add, ALU.mult
            )
        u2 = keep.tile([P, G], F32, name="u2")
        nc.vector.tensor_tensor(u2[:], u[:], u[:], ALU.mult)
        pieces = [(0, 24), (24, 24), (48, 16)]
        nda = keep.tile([P, J], F32, name="nda")

        def gradient(n):
            g0, ng = pieces[n]
            cols = slice(g0 * S, (g0 + ng) * S)
            nc.vector.scalar_tensor_tensor(
                grouped(nda[:, cols]), u2[:, g0 : g0 + ng].unsqueeze(2).to_broadcast([P, ng, S]), 1.0,
                grouped(w[:, cols]), ALU.subtract, ALU.mult,
            )

        def finish(n):
            g0, ng = pieces[n]
            cols = slice(g0 * S, (g0 + ng) * S)
            res = keep.tile([P, ng * S], F32, name="res%d" % n)
            nc.vector.scalar_tensor_tensor(res[:], nda[:, cols], -1.0 / S, old_t[:, cols], ALU.mult, ALU.add)
            nc.sync.dma_start(out[:, cols], res[:])

        gradient(0)
        gradient(1)
        finish(0)
        gradient(2)
        finish(1)
        finish(2)
